import numpy as np, ml_dtypes
CORES = [12,28,60,100,156,228]
N = 6
PG, W, NP = 2, 128, 32
def entries(a): return a.T.reshape(-1)
def pack(v, P): return np.ascontiguousarray(np.asarray(v, np.int32).reshape(-1, P).T)
def lists(rng, how):
    I = rng.integers(0, N * PG, (N, NP))
    if how == "alike": I[:] = rng.integers(0, N * PG, (N, 1))
    if how == "hotrank": I = PG * int(rng.integers(N)) + rng.integers(0, PG, (N, NP))
    if how == "own": I = PG * np.arange(N).reshape(N, 1) + rng.integers(0, PG, (N, NP))
    if how == "edge": I = PG * rng.integers(0, N, (N, NP)) + np.where(rng.random((N, NP)) < 0.5, 0, PG - 1)
    if how == "swap": s = int(rng.integers(1, N)); I = np.stack([PG * ((r + s) % N) + np.concatenate([rng.permutation(PG), rng.integers(0, PG, NP)])[:NP] for r in range(N)])
    return {"pt": np.stack([pack(I[r], 16) for r in range(N)])}
def setup_inputs(rng):
    return dict({"pool": rng.standard_normal((N, PG * 128, W), dtype=np.float32).astype(ml_dtypes.bfloat16)}, **lists(rng, "uniform"))
def setup_inputs_alike(rng):
    d = setup_inputs(rng); d.update(lists(rng, "alike"))
    for k in ("pool",): d[k] = (d[k].astype(np.float32) * 1048576.0).astype(d[k].dtype)
    return d
def setup_inputs_edge(rng):
    d = setup_inputs(rng); d.update(lists(rng, "edge"))
    for k in ("pool",): d[k] = (d[k].astype(np.float32) * (1 / 1024.0)).astype(d[k].dtype)
    return d
def setup_inputs_hotrank(rng):
    d = setup_inputs(rng); d.update(lists(rng, "hotrank"))
    return d
def setup_inputs_own(rng):
    d = setup_inputs(rng); d.update(lists(rng, "own"))
    return d
def setup_inputs_swap(rng):
    d = setup_inputs(rng); d.update(lists(rng, "swap"))
    return d
def check_inputs(x):
    bad = []
    if x["pt"].min() < 0 or x["pt"].max() >= N * PG: bad.append("pt out of range")
    return bad
def reference(pool, pt):
    A = np.concatenate(list(pool), axis=0).reshape(N * PG, 128, W)
    return {"y": np.stack([A[entries(pt[r])].reshape(NP * 128, W) for r in range(N)])}

@@ -1,0 +1,138 @@
+from concourse.bass import DstId, RemoteDMATransfer, IndirectOffsetOnAxis
+
+N, PG, NP = 6, 2, 32
+PAGE = 128 * 128
+SIM_CORES = 256
+
+SCRATCH = {
+    "land": ("dram", [N, 128, 256], "bfloat16"),
+    "table": ("dram", [N * PG, PAGE], "bfloat16"),
+    "ptS": ("sbuf", [16, 2], "int32"),
+    "big": ("sbuf", [NP, PAGE], "bfloat16"),
+}
+SEMAPHORES = ["ld", "tab", "ptl", "arrE", "arrL", "hin", "sent", "g1", "g2", "st"]
+
+
+def _bits(m):
+    return [i for i in range(16) if (m >> i) & 1]
+
+
+def _mask(es):
+    return sum(1 << e for e in es)
+
+
+def _plan(T, topo):
+    cores = list(T.cores)
+    plan = []
+    for src in cores:
+        same = [d for d in cores if d != src and topo.same_plane(src, d)]
+        cross = [d for d in cores if d != src and d not in same]
+        mates = [c for c in range(SIM_CORES)
+                 if topo.host(c) == topo.host(src) and topo.chip(c) == topo.chip(src) and c not in cores]
+        cands = [c for c in mates if all(topo.may_write(c, d) for d in cross)]
+        cands.sort(key=lambda c: (topo.die(c) != topo.die(src), c))
+        helpers = cands[:2]
+        serve = [(h, cross[i::len(helpers)]) for i, h in enumerate(helpers)]
+        plan.append({"same": same, "help": [(h, ds) for h, ds in serve if ds]})
+    return plan
+
+
+def _helper_engines(topo, h, ds):
+    off = _bits(topo.mask(h, ds[0]))
+    per = len(off) // len(ds)
+    return [off[i * per:(i + 1) * per] for i in range(len(ds))]
+
+
+def _dst(topo, d, src):
+    rid, pid = topo.addr(d, src)
+    return DstId(rid=rid, pnc=pid)
+
+
+def rank_program(g, core, T, topo):
+    plan = _plan(T, topo)
+    cores = list(T.cores)
+    rank = T.rank_of(core)
+
+    if rank is None:
+        for s, p in enumerate(plan):
+            for h, ds in p["help"]:
+                if h != core:
+                    continue
+                sets = _helper_engines(topo, h, ds)
+                n_in = len(_rank_help_engines(topo, cores[s], p)[0])
+                g.wait_ge(T.sem.hin, n_in)
+                g.remote_dma_fused(
+                    [RemoteDMATransfer(dst_ids=[_dst(topo, d, core)], dma_engine_mask=_mask(es),
+                                       remote_sem=T.sem.arrL, src=T.land[s], dst=T.land[s])
+                     for d, es in zip(ds, sets)],
+                    local_sem=T.sem.sent)
+                g.wait_ge(T.sem.sent, sum(len(es) for es in sets))
+        return
+
+    p = plan[rank]
+    g.sync.dma_start(T.land[rank], T.pool[:, :]).then_inc(T.sem.ld, 16)
+    g.scalar.dma_start(T.table[PG * rank:PG * rank + PG, :], T.pool[:, :]).then_inc(T.sem.tab, 16)
+    n_copies = 1
+
+    g.wait_ge(T.sem.ld, 16)
+    hsets = _rank_help_engines(topo, core, p)
+    g.remote_dma_fused(
+        [RemoteDMATransfer(dst_ids=[_dst(topo, h, core)], dma_engine_mask=_mask(es),
+                           remote_sem=T.sem.hin, src=T.land[rank], dst=T.land[rank])
+         for (h, _), es in zip(p["help"], hsets)],
+        local_sem=T.sem.sent)
+    sent = sum(len(es) for es in hsets)
+    off = _bits(topo.mask(core, p["same"][0]))
+    g.remote_dma_fused(
+        [RemoteDMATransfer(dst_ids=[_dst(topo, d, core) for d in p["same"]], dma_engine_mask=_mask(off),
+                           remote_sem=T.sem.arrE, srcs=[T.land[rank]], dsts=[T.land[rank] for _ in p["same"]])],
+        local_sem=T.sem.sent)
+    sent += len(off)
+    g.dma_start(T.ptS[:, :], T.pt[:, :]).then_inc(T.sem.ptl, 16)
+
+    early = [s for s in range(N) if core in plan[s]["same"]]
+    late = [s for s in range(N) if s != rank and s not in early]
+    n_early = sum(len(_bits(topo.mask(cores[s], core))) for s in early)
+    n_late = 0
+    for s in late:
+        for h, ds in plan[s]["help"]:
+            if core in ds:
+                n_late += len(_helper_engines(topo, h, ds)[ds.index(core)])
+
+    def runs(ss):
+        out = []
+        for s in ss:
+            if out and out[-1][1] == s:
+                out[-1][1] = s + 1
+            else:
+                out.append([s, s + 1])
+        return out
+
+    queues = [g.sync, g.scalar]
+    for sem, need, group in ((T.sem.arrE, n_early, early), (T.sem.arrL, n_late, late)):
+        rs = runs(group)
+        used = queues[:min(len(rs), 2)]
+        for q in used:
+            q.wait_ge(sem, need)
+        for i, (a, b) in enumerate(rs):
+            used[i % len(used)].dma_start(T.table[PG * a:PG * b, :], T.land[a:b]).then_inc(T.sem.tab, 16)
+            n_copies += 1
+
+    g.wait_ge(T.sem.ptl, 16)
+    g.wait_ge(T.sem.tab, 16 * n_copies)
+    half = NP // 2
+    for j, (gs, q) in enumerate(((T.sem.g1, g.sync), (T.sem.g2, g.scalar))):
+        g.indirect_dma_start(T.big[half * j:half * (j + 1), :], None, T.table[:],
+                             IndirectOffsetOnAxis(ap=T.ptS[:, j:j + 1], axis=0),
+                             bounds_check=N * PG - 1).then_inc(gs, 16)
+        q.wait_ge(gs, 16)
+        q.dma_start(T.y[half * 128 * j:half * 128 * (j + 1), :], T.big[half * j:half * (j + 1), :]).then_inc(T.sem.st, 16)
+    g.wait_ge(T.sem.sent, sent)
+    g.wait_ge(T.sem.st, 32)
+
+
+def _rank_help_engines(topo, core, p):
+    off = _bits(topo.mask(core, p["same"][0]))
+    on = [e for e in _bits(topo.mask(core, p["help"][0][0])) if e not in off]
+    per = len(on) // len(p["help"])
+    return [on[i * per:(i + 1) * per] for i in range(len(p["help"]))]

@@ -2,10 +2,11 @@ from concourse.bass import DstId, RemoteDMATransfer, IndirectOffsetOnAxis
 
 N, PG, NP = 6, 2, 32
 PAGE = 128 * 128
+NQ = 4
 SIM_CORES = 256
 
 SCRATCH = {
-    "land": ("dram", [N, 128, 256], "bfloat16"),
+    "land": ("dram", [N * NQ, 128, PG * PAGE // (NQ * 128)], "bfloat16"),
     "table": ("dram", [N * PG, PAGE], "bfloat16"),
     "ptS": ("sbuf", [16, 2], "int32"),
     "big": ("sbuf", [NP, PAGE], "bfloat16"),
@@ -27,20 +28,28 @@ def _plan(T, topo):
     for src in cores:
         same = [d for d in cores if d != src and topo.same_plane(src, d)]
         cross = [d for d in cores if d != src and d not in same]
-        mates = [c for c in range(SIM_CORES)
-                 if topo.host(c) == topo.host(src) and topo.chip(c) == topo.chip(src) and c not in cores]
-        cands = [c for c in mates if all(topo.may_write(c, d) for d in cross)]
+        chipmates = [c for c in range(SIM_CORES)
+                     if topo.host(c) == topo.host(src) and topo.chip(c) == topo.chip(src) and c not in cores]
+        cands = [c for c in chipmates if all(topo.may_write(c, d) for d in cross)]
         cands.sort(key=lambda c: (topo.die(c) != topo.die(src), c))
-        helpers = cands[:2]
-        serve = [(h, cross[i::len(helpers)]) for i, h in enumerate(helpers)]
-        plan.append({"same": same, "help": [(h, ds) for h, ds in serve if ds]})
+        plan.append({"same": same, "cross": cross, "help": cands[:NQ]})
     return plan
 
 
 def _helper_engines(topo, h, ds):
-    off = _bits(topo.mask(h, ds[0]))
-    per = len(off) // len(ds)
-    return [off[i * per:(i + 1) * per] for i in range(len(ds))]
+    return _bits(topo.mask(h, ds[0]))[::2][:len(ds)]
+
+
+def _rank_help_engines(topo, core, p):
+    off = _bits(topo.mask(core, p["same"][0]))
+    on = [e for e in _bits(topo.mask(core, p["help"][0])) if e not in off]
+    return on[::2][:len(p["help"])]
+
+
+def _same_engines(topo, core, p):
+    off = _bits(topo.mask(core, p["same"][0]))
+    per = len(off) // NQ
+    return [off[i * per:(i + 1) * per] for i in range(NQ)]
 
 
 def _dst(topo, d, src):
@@ -55,49 +64,47 @@ def rank_program(g, core, T, topo):
 
     if rank is None:
         for s, p in enumerate(plan):
-            for h, ds in p["help"]:
-                if h != core:
-                    continue
-                sets = _helper_engines(topo, h, ds)
-                n_in = len(_rank_help_engines(topo, cores[s], p)[0])
-                g.wait_ge(T.sem.hin, n_in)
-                g.remote_dma_fused(
-                    [RemoteDMATransfer(dst_ids=[_dst(topo, d, core)], dma_engine_mask=_mask(es),
-                                       remote_sem=T.sem.arrL, src=T.land[s], dst=T.land[s])
-                     for d, es in zip(ds, sets)],
-                    local_sem=T.sem.sent)
-                g.wait_ge(T.sem.sent, sum(len(es) for es in sets))
+            if core not in p["help"]:
+                continue
+            blk = NQ * s + p["help"].index(core)
+            ds = p["cross"]
+            es = _helper_engines(topo, core, ds)
+            g.wait_ge(T.sem.hin, 1)
+            g.remote_dma_fused(
+                [RemoteDMATransfer(dst_ids=[_dst(topo, d, core)], dma_engine_mask=_mask([e]),
+                                   remote_sem=T.sem.arrL, src=T.land[blk], dst=T.land[blk])
+                 for d, e in zip(ds, es)],
+                local_sem=T.sem.sent)
+            g.wait_ge(T.sem.sent, len(ds))
         return
 
     p = plan[rank]
-    g.sync.dma_start(T.land[rank], T.pool[:, :]).then_inc(T.sem.ld, 16)
+    g.sync.dma_start(T.land[NQ * rank:NQ * rank + NQ], T.pool[:, :]).then_inc(T.sem.ld, 16)
     g.scalar.dma_start(T.table[PG * rank:PG * rank + PG, :], T.pool[:, :]).then_inc(T.sem.tab, 16)
     n_copies = 1
 
     g.wait_ge(T.sem.ld, 16)
-    hsets = _rank_help_engines(topo, core, p)
+    hes = _rank_help_engines(topo, core, p)
     g.remote_dma_fused(
-        [RemoteDMATransfer(dst_ids=[_dst(topo, h, core)], dma_engine_mask=_mask(es),
-                           remote_sem=T.sem.hin, src=T.land[rank], dst=T.land[rank])
-         for (h, _), es in zip(p["help"], hsets)],
+        [RemoteDMATransfer(dst_ids=[_dst(topo, h, core)], dma_engine_mask=_mask([e]),
+                           remote_sem=T.sem.hin, src=T.land[NQ * rank + j], dst=T.land[NQ * rank + j])
+         for j, (h, e) in enumerate(zip(p["help"], hes))],
         local_sem=T.sem.sent)
-    sent = sum(len(es) for es in hsets)
-    off = _bits(topo.mask(core, p["same"][0]))
+    sent = len(hes)
+    ssets = _same_engines(topo, core, p)
     g.remote_dma_fused(
-        [RemoteDMATransfer(dst_ids=[_dst(topo, d, core) for d in p["same"]], dma_engine_mask=_mask(off),
-                           remote_sem=T.sem.arrE, srcs=[T.land[rank]], dsts=[T.land[rank] for _ in p["same"]])],
+        [RemoteDMATransfer(dst_ids=[_dst(topo, d, core) for d in p["same"]], dma_engine_mask=_mask(es),
+                           remote_sem=T.sem.arrE, srcs=[T.land[NQ * rank + j]],
+                           dsts=[T.land[NQ * rank + j] for _ in p["same"]])
+         for j, es in enumerate(ssets)],
         local_sem=T.sem.sent)
-    sent += len(off)
+    sent += sum(len(es) for es in ssets)
     g.dma_start(T.ptS[:, :], T.pt[:, :]).then_inc(T.sem.ptl, 16)
 
     early = [s for s in range(N) if core in plan[s]["same"]]
-    late = [s for s in range(N) if s != rank and s not in early]
-    n_early = sum(len(_bits(topo.mask(cores[s], core))) for s in early)
-    n_late = 0
-    for s in late:
-        for h, ds in plan[s]["help"]:
-            if core in ds:
-                n_late += len(_helper_engines(topo, h, ds)[ds.index(core)])
+    late = [s for s in range(N) if core in plan[s]["cross"]]
+    n_early = sum(sum(len(es) for es in _same_engines(topo, cores[s], plan[s])) for s in early)
+    n_late = sum(len(plan[s]["help"]) for s in late)
 
     def runs(ss):
         out = []
@@ -115,7 +122,7 @@ def rank_program(g, core, T, topo):
         for q in used:
             q.wait_ge(sem, need)
         for i, (a, b) in enumerate(rs):
-            used[i % len(used)].dma_start(T.table[PG * a:PG * b, :], T.land[a:b]).then_inc(T.sem.tab, 16)
+            used[i % len(used)].dma_start(T.table[PG * a:PG * b, :], T.land[NQ * a:NQ * b]).then_inc(T.sem.tab, 16)
             n_copies += 1
 
     g.wait_ge(T.sem.ptl, 16)
@@ -129,10 +136,3 @@ def rank_program(g, core, T, topo):
         q.dma_start(T.y[half * 128 * j:half * 128 * (j + 1), :], T.big[half * j:half * (j + 1), :]).then_inc(T.sem.st, 16)
     g.wait_ge(T.sem.sent, sent)
     g.wait_ge(T.sem.st, 32)
-
-
-def _rank_help_engines(topo, core, p):
-    off = _bits(topo.mask(core, p["same"][0]))
-    on = [e for e in _bits(topo.mask(core, p["help"][0][0])) if e not in off]
-    per = len(on) // len(p["help"])
-    return [on[i * per:(i + 1) * per] for i in range(len(p["help"]))]

@@ -1,17 +1,26 @@
 from concourse.bass import DstId, RemoteDMATransfer, IndirectOffsetOnAxis
+from concourse.mybir import AluOpType
 
 N, PG, NP = 6, 2, 32
 PAGE = 128 * 128
 NQ = 4
+NH = 2
+NB = NQ * NH
+QP = 4
+E1 = 20
+PTR = 16
 SIM_CORES = 256
 
 SCRATCH = {
-    "land": ("dram", [N * NQ, 128, PG * PAGE // (NQ * 128)], "bfloat16"),
-    "table": ("dram", [N * PG, PAGE], "bfloat16"),
-    "ptS": ("sbuf", [16, 2], "int32"),
-    "big": ("sbuf", [NP, PAGE], "bfloat16"),
+    "land": ("dram", [N * NB, 128, PG * PAGE // (NB * 128)], "bfloat16"),
+    "table": ("dram", [N * PG * QP, PAGE // QP], "bfloat16"),
+    "ptS": ("sbuf", [PTR, 2], "int32"),
+    "qv": ("sbuf", [PTR, 2 * QP], "int32"),
+    "i1": ("sbuf", [E1 * QP, 1], "int32"),
+    "i2": ("sbuf", [(NP - E1) * QP, 1], "int32"),
+    "big": ("sbuf", [NP * QP, PAGE // QP], "bfloat16"),
 }
-SEMAPHORES = ["ld", "tab", "ptl", "arrE", "arrL", "hin", "sent", "g1", "g2", "st"]
+SEMAPHORES = ["ld", "tab", "pl", "vs", "ix", "ptl", "arrE", "arrL0", "arrL1", "hin0", "hin1", "sent", "g1", "g2", "st"]
 
 
 def _bits(m):
@@ -40,16 +49,17 @@ def _helper_engines(topo, h, ds):
     return _bits(topo.mask(h, ds[0]))[::2][:len(ds)]
 
 
-def _rank_help_engines(topo, core, p):
+def _rank_help_engines(topo, core, p, h):
     off = _bits(topo.mask(core, p["same"][0]))
-    on = [e for e in _bits(topo.mask(core, p["help"][0])) if e not in off]
-    return on[::2][:len(p["help"])]
+    on = _bits(topo.mask(core, p["help"][0]))
+    pick = [e for e in on if e in off] if h == 0 else [e for e in on if e not in off]
+    return pick[::2][:len(p["help"])]
 
 
 def _same_engines(topo, core, p):
     off = _bits(topo.mask(core, p["same"][0]))
-    per = len(off) // NQ
-    return [off[i * per:(i + 1) * per] for i in range(NQ)]
+    per = len(off) // NB
+    return [off[i * per:(i + 1) * per] for i in range(NB)]
 
 
 def _dst(topo, d, src):
@@ -66,40 +76,62 @@ def rank_program(g, core, T, topo):
         for s, p in enumerate(plan):
             if core not in p["help"]:
                 continue
-            blk = NQ * s + p["help"].index(core)
             ds = p["cross"]
             es = _helper_engines(topo, core, ds)
-            g.wait_ge(T.sem.hin, 1)
-            g.remote_dma_fused(
-                [RemoteDMATransfer(dst_ids=[_dst(topo, d, core)], dma_engine_mask=_mask([e]),
-                                   remote_sem=T.sem.arrL, src=T.land[blk], dst=T.land[blk])
-                 for d, e in zip(ds, es)],
-                local_sem=T.sem.sent)
-            g.wait_ge(T.sem.sent, len(ds))
+            for h in range(NH):
+                blk = NB * s + NH * p["help"].index(core) + h
+                g.wait_ge(T.sem["hin%d" % h], 1)
+                g.remote_dma_fused(
+                    [RemoteDMATransfer(dst_ids=[_dst(topo, d, core)], dma_engine_mask=_mask([e]),
+                                       remote_sem=T.sem["arrL%d" % h], src=T.land[blk], dst=T.land[blk])
+                     for d, e in zip(ds, es)],
+                    local_sem=T.sem.sent)
+            g.wait_ge(T.sem.sent, NH * len(ds))
         return
 
     p = plan[rank]
-    g.sync.dma_start(T.land[NQ * rank:NQ * rank + NQ], T.pool[:, :]).then_inc(T.sem.ld, 16)
-    g.scalar.dma_start(T.table[PG * rank:PG * rank + PG, :], T.pool[:, :]).then_inc(T.sem.tab, 16)
+    SR = PG * QP
+    g.sync.dma_start(T.land[NB * rank:NB * rank + NB], T.pool[:, :]).then_inc(T.sem.ld, 16)
+    g.scalar.dma_start(T.ptS[:, :], T.pt[:, :]).then_inc(T.sem.pl, 16)
+    g.scalar.dma_start(T.table[SR * rank:SR * rank + SR, :], T.pool[:, :]).then_inc(T.sem.tab, 16)
     n_copies = 1
 
+    g.vector.wait_ge(T.sem.pl, 16)
+    for j in range(2):
+        for q in range(QP):
+            c = QP * j + q
+            g.vector.tensor_scalar(T.qv[:, c:c + 1], T.ptS[:, j:j + 1], float(QP), float(q),
+                                   AluOpType.mult, AluOpType.add).then_inc(T.sem.vs, 1)
+    g.sync.wait_ge(T.sem.vs, 2 * QP)
+    g.sync.dma_start(T.i1[0:PTR * QP, :], T.qv[:, 0:QP]).then_inc(T.sem.ix, 16)
+    g.sync.dma_start(T.i1[PTR * QP:E1 * QP, :], T.qv[0:E1 - PTR, QP:2 * QP]).then_inc(T.sem.ix, 16)
+
     g.wait_ge(T.sem.ld, 16)
-    hes = _rank_help_engines(topo, core, p)
-    g.remote_dma_fused(
-        [RemoteDMATransfer(dst_ids=[_dst(topo, h, core)], dma_engine_mask=_mask([e]),
-                           remote_sem=T.sem.hin, src=T.land[NQ * rank + j], dst=T.land[NQ * rank + j])
-         for j, (h, e) in enumerate(zip(p["help"], hes))],
-        local_sem=T.sem.sent)
-    sent = len(hes)
+    sent = 0
+
+    def to_helpers(h):
+        hes = _rank_help_engines(topo, core, p, h)
+        g.remote_dma_fused(
+            [RemoteDMATransfer(dst_ids=[_dst(topo, c, core)], dma_engine_mask=_mask([e]),
+                               remote_sem=T.sem["hin%d" % h],
+                               src=T.land[NB * rank + NH * j + h], dst=T.land[NB * rank + NH * j + h])
+             for j, (c, e) in enumerate(zip(p["help"], hes))],
+            local_sem=T.sem.sent)
+        return len(hes)
+
+    sent += to_helpers(0)
     ssets = _same_engines(topo, core, p)
     g.remote_dma_fused(
         [RemoteDMATransfer(dst_ids=[_dst(topo, d, core) for d in p["same"]], dma_engine_mask=_mask(es),
-                           remote_sem=T.sem.arrE, srcs=[T.land[NQ * rank + j]],
-                           dsts=[T.land[NQ * rank + j] for _ in p["same"]])
-         for j, es in enumerate(ssets)],
+                           remote_sem=T.sem.arrE, srcs=[T.land[NB * rank + b]],
+                           dsts=[T.land[NB * rank + b] for _ in p["same"]])
+         for b, es in enumerate(ssets)],
         local_sem=T.sem.sent)
     sent += sum(len(es) for es in ssets)
-    g.dma_start(T.ptS[:, :], T.pt[:, :]).then_inc(T.sem.ptl, 16)
+    for h in range(1, NH):
+        sent += to_helpers(h)
+    g.wait_ge(T.sem.vs, 2 * QP)
+    g.dma_start(T.i2[:, :], T.qv[E1 - PTR:PTR, QP:2 * QP]).then_inc(T.sem.ptl, 16)
 
     early = [s for s in range(N) if core in plan[s]["same"]]
     late = [s for s in range(N) if core in plan[s]["cross"]]
@@ -116,23 +148,26 @@ def rank_program(g, core, T, topo):
         return out
 
     queues = [g.sync, g.scalar]
-    for sem, need, group in ((T.sem.arrE, n_early, early), (T.sem.arrL, n_late, late)):
+    waves = [(T.sem.arrE, n_early, early, 0, 1)]
+    waves += [(T.sem["arrL%d" % h], n_late, late, h, NH) for h in range(NH)]
+    for sem, need, group, first, step in waves:
         rs = runs(group)
         used = queues[:min(len(rs), 2)]
         for q in used:
             q.wait_ge(sem, need)
         for i, (a, b) in enumerate(rs):
-            used[i % len(used)].dma_start(T.table[PG * a:PG * b, :], T.land[NQ * a:NQ * b]).then_inc(T.sem.tab, 16)
+            used[i % len(used)].dma_start(T.table[SR * a + first:SR * b:step, :],
+                                          T.land[NB * a + first:NB * b:step]).then_inc(T.sem.tab, 16)
             n_copies += 1
 
     g.wait_ge(T.sem.ptl, 16)
+    g.wait_ge(T.sem.ix, 32)
     g.wait_ge(T.sem.tab, 16 * n_copies)
-    half = NP // 2
-    for j, (gs, q) in enumerate(((T.sem.g1, g.sync), (T.sem.g2, g.scalar))):
-        g.indirect_dma_start(T.big[half * j:half * (j + 1), :], None, T.table[:],
-                             IndirectOffsetOnAxis(ap=T.ptS[:, j:j + 1], axis=0),
-                             bounds_check=N * PG - 1).then_inc(gs, 16)
+    for (a, b), idx, gs, q in (((0, E1), T.i1, T.sem.g1, g.sync), ((E1, NP), T.i2, T.sem.g2, g.scalar)):
+        g.indirect_dma_start(T.big[QP * a:QP * b, :], None, T.table[:],
+                             IndirectOffsetOnAxis(ap=idx[:, 0:1], axis=0),
+                             bounds_check=N * PG * QP - 1).then_inc(gs, 16)
         q.wait_ge(gs, 16)
-        q.dma_start(T.y[half * 128 * j:half * 128 * (j + 1), :], T.big[half * j:half * (j + 1), :]).then_inc(T.sem.st, 16)
+        q.dma_start(T.y[128 * a:128 * b, :], T.big[QP * a:QP * b, :]).then_inc(T.sem.st, 16)
     g.wait_ge(T.sem.sent, sent)
     g.wait_ge(T.sem.st, 32)

from concourse.bass import DstId, RemoteDMATransfer, IndirectOffsetOnAxis
from concourse.mybir import AluOpType

N, PG, NP = 6, 2, 32
PAGE = 128 * 128
NQ = 4
NH = 2
NB = NQ * NH
QP = 4
E1 = 20
PTR = 16
SIM_CORES = 256

SCRATCH = {
    "land": ("dram", [N * NB, 128, PG * PAGE // (NB * 128)], "bfloat16"),
    "table": ("dram", [N * PG * QP, PAGE // QP], "bfloat16"),
    "ptS": ("sbuf", [PTR, 2], "int32"),
    "qv": ("sbuf", [PTR, 2 * QP], "int32"),
    "i1": ("sbuf", [E1 * QP, 1], "int32"),
    "i2": ("sbuf", [(NP - E1) * QP, 1], "int32"),
    "big": ("sbuf", [NP * QP, PAGE // QP], "bfloat16"),
}
SEMAPHORES = ["ld", "tab", "pl", "vs", "ix", "ptl", "arrE", "arrL0", "arrL1", "hin0", "hin1", "sent", "g1", "g2", "st"]


def _bits(m):
    return [i for i in range(16) if (m >> i) & 1]


def _mask(es):
    return sum(1 << e for e in es)


def _plan(T, topo):
    cores = list(T.cores)
    plan = []
    for src in cores:
        same = [d for d in cores if d != src and topo.same_plane(src, d)]
        cross = [d for d in cores if d != src and d not in same]
        chipmates = [c for c in range(SIM_CORES)
                     if topo.host(c) == topo.host(src) and topo.chip(c) == topo.chip(src) and c not in cores]
        cands = [c for c in chipmates if all(topo.may_write(c, d) for d in cross)]
        cands.sort(key=lambda c: (topo.die(c) != topo.die(src), c))
        plan.append({"same": same, "cross": cross, "help": cands[:NQ]})
    return plan


def _helper_engines(topo, h, ds):
    return _bits(topo.mask(h, ds[0]))[::2][:len(ds)]


def _rank_help_engines(topo, core, p, h):
    off = _bits(topo.mask(core, p["same"][0]))
    on = _bits(topo.mask(core, p["help"][0]))
    pick = [e for e in on if e in off] if h == 0 else [e for e in on if e not in off]
    return pick[::2][:len(p["help"])]


def _same_engines(topo, core, p):
    off = _bits(topo.mask(core, p["same"][0]))
    per = len(off) // NB
    return [off[i * per:(i + 1) * per] for i in range(NB)]


def _dst(topo, d, src):
    rid, pid = topo.addr(d, src)
    return DstId(rid=rid, pnc=pid)


def rank_program(g, core, T, topo):
    plan = _plan(T, topo)
    cores = list(T.cores)
    rank = T.rank_of(core)

    if rank is None:
        for s, p in enumerate(plan):
            if core not in p["help"]:
                continue
            ds = p["cross"]
            es = _helper_engines(topo, core, ds)
            for h in range(NH):
                blk = NB * s + NH * p["help"].index(core) + h
                g.wait_ge(T.sem["hin%d" % h], 1)
                g.remote_dma_fused(
                    [RemoteDMATransfer(dst_ids=[_dst(topo, d, core)], dma_engine_mask=_mask([e]),
                                       remote_sem=T.sem["arrL%d" % h], src=T.land[blk], dst=T.land[blk])
                     for d, e in zip(ds, es)],
                    local_sem=T.sem.sent)
            g.wait_ge(T.sem.sent, NH * len(ds))
        return

    p = plan[rank]
    SR = PG * QP
    g.sync.dma_start(T.land[NB * rank:NB * rank + NB], T.pool[:, :]).then_inc(T.sem.ld, 16)
    g.scalar.dma_start(T.ptS[:, :], T.pt[:, :]).then_inc(T.sem.pl, 16)
    g.scalar.dma_start(T.table[SR * rank:SR * rank + SR, :], T.pool[:, :]).then_inc(T.sem.tab, 16)
    n_copies = 1

    g.vector.wait_ge(T.sem.pl, 16)
    for j in range(2):
        for q in range(QP):
            c = QP * j + q
            g.vector.tensor_scalar(T.qv[:, c:c + 1], T.ptS[:, j:j + 1], float(QP), float(q),
                                   AluOpType.mult, AluOpType.add).then_inc(T.sem.vs, 1)
    g.sync.wait_ge(T.sem.vs, 2 * QP)
    g.sync.dma_start(T.i1[0:PTR * QP, :], T.qv[:, 0:QP]).then_inc(T.sem.ix, 16)
    g.sync.dma_start(T.i1[PTR * QP:E1 * QP, :], T.qv[0:E1 - PTR, QP:2 * QP]).then_inc(T.sem.ix, 16)

    g.wait_ge(T.sem.ld, 16)
    sent = 0

    def to_helpers(h):
        hes = _rank_help_engines(topo, core, p, h)
        g.remote_dma_fused(
            [RemoteDMATransfer(dst_ids=[_dst(topo, c, core)], dma_engine_mask=_mask([e]),
                               remote_sem=T.sem["hin%d" % h],
                               src=T.land[NB * rank + NH * j + h], dst=T.land[NB * rank + NH * j + h])
             for j, (c, e) in enumerate(zip(p["help"], hes))],
            local_sem=T.sem.sent)
        return len(hes)

    sent += to_helpers(0)
    ssets = _same_engines(topo, core, p)
    g.remote_dma_fused(
        [RemoteDMATransfer(dst_ids=[_dst(topo, d, core) for d in p["same"]], dma_engine_mask=_mask(es),
                           remote_sem=T.sem.arrE, srcs=[T.land[NB * rank + b]],
                           dsts=[T.land[NB * rank + b] for _ in p["same"]])
         for b, es in enumerate(ssets)],
        local_sem=T.sem.sent)
    sent += sum(len(es) for es in ssets)
    for h in range(1, NH):
        sent += to_helpers(h)
    g.wait_ge(T.sem.vs, 2 * QP)
    g.dma_start(T.i2[:, :], T.qv[E1 - PTR:PTR, QP:2 * QP]).then_inc(T.sem.ptl, 16)

    early = [s for s in range(N) if core in plan[s]["same"]]
    late = [s for s in range(N) if core in plan[s]["cross"]]
    n_early = sum(sum(len(es) for es in _same_engines(topo, cores[s], plan[s])) for s in early)
    n_late = sum(len(plan[s]["help"]) for s in late)

    def runs(ss):
        out = []
        for s in ss:
            if out and out[-1][1] == s:
                out[-1][1] = s + 1
            else:
                out.append([s, s + 1])
        return out

    queues = [g.sync, g.scalar]
    waves = [(T.sem.arrE, n_early, early, 0, 1)]
    waves += [(T.sem["arrL%d" % h], n_late, late, h, NH) for h in range(NH)]
    for sem, need, group, first, step in waves:
        rs = runs(group)
        used = queues[:min(len(rs), 2)]
        for q in used:
            q.wait_ge(sem, need)
        for i, (a, b) in enumerate(rs):
            used[i % len(used)].dma_start(T.table[SR * a + first:SR * b:step, :],
                                          T.land[NB * a + first:NB * b:step]).then_inc(T.sem.tab, 16)
            n_copies += 1

    g.wait_ge(T.sem.ptl, 16)
    g.wait_ge(T.sem.ix, 32)
    g.wait_ge(T.sem.tab, 16 * n_copies)
    for (a, b), idx, gs, q in (((0, E1), T.i1, T.sem.g1, g.sync), ((E1, NP), T.i2, T.sem.g2, g.scalar)):
        g.indirect_dma_start(T.big[QP * a:QP * b, :], None, T.table[:],
                             IndirectOffsetOnAxis(ap=idx[:, 0:1], axis=0),
                             bounds_check=N * PG * QP - 1).then_inc(gs, 16)
        q.wait_ge(gs, 16)
        q.dma_start(T.y[128 * a:128 * b, :], T.big[QP * a:QP * b, :]).then_inc(T.sem.st, 16)
    g.wait_ge(T.sem.sent, sent)
    g.wait_ge(T.sem.st, 32)
